import numpy as np
import ml_dtypes


def mxq(x, axis, fmt="e4m3"):
    dtype, down = {"e4m3": (ml_dtypes.float8_e4m3fn, 7), "e5m2": (ml_dtypes.float8_e5m2, 14)}[fmt]
    v = np.moveaxis(np.asarray(x, np.float32).astype(ml_dtypes.bfloat16).astype(np.float64), axis, -1)
    blocks = v.reshape(v.shape[:-1] + (-1, 32))
    amax = np.abs(blocks).max(-1, keepdims=True)
    byte = np.maximum(np.where(amax > 0, np.frexp(amax)[1] - 1 + 127, 0) - down, 1)
    scale = np.exp2(byte - 127.0)
    codes = (blocks / scale).astype(np.float32).astype(dtype).astype(np.float64)
    return np.moveaxis((codes * scale).reshape(v.shape), -1, axis)


WIDE = False


def mx_kscale(k):
    if not WIDE:
        return np.ones(k)
    levels = np.array([30, -30])
    if k % 512:
        return np.exp2(np.random.permutation(np.resize(levels, k // 32))).repeat(32)
    a = np.empty((k // 512, 16))
    for p in range(k // 512):
        a[p, :8] = np.random.permutation(np.resize(levels, 8))
        for g in range(8):
            far = levels[np.abs(levels - a[p, g]) >= 10]
            a[p, g + 8] = far[np.random.randint(len(far))]
    return np.exp2(a.ravel()).repeat(32)


def f64(x):
    return np.asarray(x).astype(np.float64)


def striped(idx):
    return np.tile(np.asarray(idx).reshape(-1, 16).T, (8, 1)).astype(np.uint16)


def unstriped(offs):
    return offs[:16].T.reshape(-1).astype(np.int64)


E2M1 = np.array([0.0, 0.5, 1.0, 1.5, 2.0, 3.0, 4.0, 6.0, -0.0, -0.5, -1.0, -1.5, -2.0, -3.0, -4.0, -6.0])


def pack_weight(w, fmt):
    k, n = w.shape
    w = f64(np.asarray(w, np.float32).astype(ml_dtypes.bfloat16)).reshape(k // 32, 32, n)
    amax = np.abs(w).max(1)
    if fmt in ("e4m3", "e5m2"):
        byte = np.frexp(amax)[1] - 1 + 127 - (7 if fmt == "e4m3" else 14)
    else:
        mant, ex = np.frexp(amax / 6.0)
        byte = np.where(mant > 0.5, ex, ex - 1) + 127
    byte = np.clip(np.where(amax > 0, byte, 1), 1, 254)
    scaled = (w * np.exp2(127.0 - byte)[:, None, :]).reshape(k, n).astype(np.float32)
    by_word = np.ascontiguousarray(scaled.reshape(k // 512, 128, 4, n).transpose(0, 1, 3, 2))
    if fmt in ("e4m3", "e5m2"):
        words = by_word.astype(ml_dtypes.float8_e4m3fn if fmt == "e4m3" else ml_dtypes.float8_e5m2).view(np.uint8)
    else:
        c = by_word.astype(ml_dtypes.float4_e2m1fn).view(np.uint8) & 0xF
        words = (c[..., 0::2] | (c[..., 1::2] << 4)).reshape(k // 512, 128, 2 * n)
    return np.ascontiguousarray(words), np.ascontiguousarray(byte.astype(np.uint8).reshape(k // 512, 16, n))


def unpack_weight(words, scales, fmt):
    g, _, n = scales.shape
    words = np.ascontiguousarray(words).reshape(g, 128, n, -1)
    if fmt in ("e4m3", "e5m2"):
        vals = words.view(ml_dtypes.float8_e4m3fn if fmt == "e4m3" else ml_dtypes.float8_e5m2).astype(np.float64)
    else:
        nib = np.empty((g, 128, n, 4), np.uint8)
        nib[..., 0::2] = words & 0xF
        nib[..., 1::2] = words >> 4
        vals = E2M1[nib]
    vals = vals * np.repeat(np.exp2(scales.astype(np.float64) - 127.0), 8, axis=1)[..., None]
    return vals.transpose(0, 1, 3, 2).reshape(g * 512, n)


def bf(x):
    return np.asarray(x, np.float32).astype(ml_dtypes.bfloat16)


def planes(Y):
    r, m = Y.shape
    b = f64(bf(Y)).reshape(r // 32, 32, m)
    amax = np.abs(b).max(1)
    byte = np.clip(np.where(amax > 0, np.frexp(amax)[1] - 1 + 127 - 7, 1), 1, 254)
    codes = (b * np.exp2(127.0 - byte)[:, None, :]).reshape(r, m).astype(np.float32).astype(ml_dtypes.float8_e4m3fn).view(np.uint8)
    words = codes.reshape(r // 512, 128, 4, m).transpose(0, 1, 3, 2)
    return np.ascontiguousarray(words), np.ascontiguousarray(byte.astype(np.uint8).reshape(r // 512, 16, m))


K, T, J, I, L, S, R, O, N = 512, 512, 256, 128, 128, 512, 512, 128, 512


def setup_inputs():
    n = np.random.standard_normal
    idx = np.random.permutation(T)[:I]
    idx2 = np.random.permutation(S)[:L]
    idx3 = np.random.permutation(J)[:O]
    idx4 = np.random.permutation(J)[:O]
    fk = mx_kscale(K)
    fr = mx_kscale(R)
    wp = pack_weight(n((K, R)) * 1 / np.sqrt(K) * fk[:, None] * fr, "e5m2")
    wbp = pack_weight(n((R, N)) * 1 / np.sqrt(R) / fr[:, None], "e2m1")
    return {
        "xa": (n((K, T)) / fk[:, None]).astype(np.float32),
        "xb": (n((K, S)) * 0.6 / fk[:, None]).astype(np.float32),
        "w_words": wp[0],
        "w_scales": wp[1],
        "wb_words": wbp[0],
        "wb_scales": wbp[1],
        "rs": (n((N, O))).astype(np.float32),
        "offs": striped(idx),
        "offs2": striped(idx2),
        "offs3": striped(idx3),
        "offs4": striped(idx4),
    }


def reference(xa, xb, w_words, w_scales, wb_words, wb_scales, rs, offs, offs2, offs3, offs4):
    idx = unstriped(offs)
    idx2 = unstriped(offs2)
    idx3 = unstriped(offs3)
    idx4 = unstriped(offs4)
    wu = unpack_weight(w_words, w_scales, "e5m2")
    wbu = unpack_weight(wb_words, wb_scales, "e2m1")
    u = np.concatenate([f64(xa)[:, idx], f64(xb)[:, idx2]], axis=1)
    uq = mxq(u, 0, "e5m2")
    a = wu.T @ uq
    hid = np.maximum(a[:, idx3], a[:, idx4])
    hidq = mxq(hid, 0, "e5m2")
    p = wbu.T @ hidq
    p1 = np.pad(p, ((0, 0), (1, 0)))[:, :O]
    y = p - 0.7 * p1 + 0.5 * f64(rs)
    words, scales = planes(y)
    return y, words, scales

from contextlib import ExitStack

import concourse.mybir as mybir

K, T, J, L, R, O, N = 512, 512, 256, 128, 512, 128, 512
FLOPS = 2 * K * R * J + 2 * R * N * O

F32 = mybir.dt.float32
BF16 = mybir.dt.bfloat16
I32 = mybir.dt.int32
U16 = mybir.dt.uint16
U8 = mybir.dt.uint8
E5M2 = mybir.dt.float8_e5m2_x4
E4M3 = mybir.dt.float8_e4m3fn_x4
E2M1 = mybir.dt.float4_e2m1fn_x4
ALU = mybir.AluOpType
COPY = mybir.ActivationFunctionType.Copy

P = 128
PACK = 4


def tile_list_looks_joined_larger_lagged_pl_kernel(
    tc, xa, xb, w_words, w_scales, wb_words, wb_scales, rs, offs, offs2, offs3, offs4, out_0, out_1, out_2
):
    nc = tc.nc
    with ExitStack() as ctx:
        sb = ctx.enter_context(tc.tile_pool(name="sb", bufs=1))
        ps = ctx.enter_context(tc.psum_pool(name="ps", bufs=1))

        def deal(out, raw, run):
            nc.vector.tensor_copy(
                out=out.rearrange("p (t c i) -> p c t i", t=PACK, i=run),
                in_=raw.rearrange("p (c i t) -> p c t i", t=PACK, i=run),
            )

        def woven(tile_bf):
            return tile_bf[:].rearrange("p (c i t) -> p c t i", t=PACK, i=4)

        def planar(tile_f32):
            return tile_f32[:].rearrange("p t (c i) -> p c t i", i=4)

        xa_v = xa.rearrange("(p t) c -> p t c", t=PACK)
        xb_v = xb.rearrange("(p t) c -> p t c", t=PACK)

        ws_raw = sb.tile([P, R], U8, name="ws_raw")
        wbs_raw = sb.tile([P, N], U8, name="wbs_raw")
        nc.vector.memset(ws_raw[:].bitcast(I32), 0)
        nc.vector.memset(wbs_raw[:].bitcast(I32), 0)
        for q in range(4):
            nc.scalar.dma_start(ws_raw[32 * q : 32 * q + 4, :].bitcast(I32), w_scales[0, 4 * q : 4 * q + 4, :].bitcast(I32))

        w_raw = sb.tile([P, R], I32, name="w_raw")
        wb_raw = sb.tile([P, 2 * N], U8, name="wb_raw")
        xa_lo = sb.tile([P, 2, T], F32, name="xa_lo")
        xa_hi = sb.tile([P, 2, T], F32, name="xa_hi")
        xb_lo = sb.tile([P, 2, T], F32, name="xb_lo")
        xb_2 = sb.tile([P, T], F32, name="xb_2")
        xb_3 = sb.tile([P, T], F32, name="xb_3")
        rs_sb = sb.tile([P, PACK, O], F32, name="rs_sb")
        l1 = sb.tile([P, L // 16], U16, name="l1")
        l2 = sb.tile([P, L // 16], U16, name="l2")
        l3 = sb.tile([P, O // 16], U16, name="l3")
        l4 = sb.tile([P, O // 16], U16, name="l4")

        nc.sync.dma_start(w_raw[:], w_words[0].rearrange("p n t -> p (n t)").bitcast(I32))
        nc.sync.dma_start(xa_lo[:], xa_v[:, 0:2, :])
        nc.sync.dma_start(l1[:], offs)
        nc.sync.dma_start(xa_hi[:], xa_v[:, 2:4, :])
        nc.sync.dma_start(xb_lo[:], xb_v[:, 0:2, :])
        nc.sync.dma_start(l2[:], offs2)
        nc.sync.dma_start(xb_2[:], xb_v[:, 2, :])
        nc.sync.dma_start(xb_3[:], xb_v[:, 3, :])
        nc.sync.dma_start(wb_raw[:].bitcast(I32), wb_words[0].bitcast(I32))
        for q in range(4):
            nc.sync.dma_start(wbs_raw[32 * q : 32 * q + 4, :].bitcast(I32), wb_scales[0, 4 * q : 4 * q + 4, :].bitcast(I32))
        nc.sync.dma_start(l3[:], offs3)
        nc.sync.dma_start(l4[:], offs4)
        nc.sync.dma_start(rs_sb[:], rs.rearrange("(p t) o -> p t o", t=PACK))

        w_q = sb.tile([P, R], I32, name="w_q", align_bytes=64)
        ws_q = sb.tile([P, R], U8, name="ws_q", align_bytes=64)
        wb_q = sb.tile([P, 2 * N], U8, name="wb_q", align_bytes=64)
        wbs_q = sb.tile([P, N], U8, name="wbs_q", align_bytes=64)
        deal(w_q[:], w_raw[:], 4)
        deal(ws_q[:], ws_raw[:], 16)

        a = [sb.tile([P, J], F32, name=f"a{t}") for t in range(PACK)]

        ga = sb.tile([P, PACK, L], F32, name="ga")
        for t in range(PACK):
            win = (xa_lo, xa_hi)[t // 2][:, t % 2, :]
            nc.scalar.activation(ga[:, t, :], win.indirect(l1[:]), COPY)
        ua_bf = sb.tile([P, PACK * L], BF16, name="ua_bf", align_bytes=64)
        nc.scalar.copy(woven(ua_bf), planar(ga))
        ua_q = sb.tile([P, L], I32, name="ua_q", align_bytes=64)
        ua_s = sb.tile([P, L], U8, name="ua_s", align_bytes=64)
        nc.vector.quantize_mx(out=ua_q[:].bitcast(E5M2), scales=ua_s[:], in_=ua_bf[:])
        pa = ps.tile([P, PACK, L], F32, name="pa")
        for t in range(PACK):
            cols = slice(t * P, (t + 1) * P)
            nc.tensor.matmul_mx(
                out=pa[:, t, :], lhsT=w_q[:, cols].bitcast(E5M2), lhsT_scale=ws_q[:, cols],
                rhs=ua_q[:].bitcast(E5M2), rhs_scale=ua_s[:], start=True, stop=True,
            )
        for t in range(PACK):
            nc.scalar.copy(a[t][:, 0:L], pa[:, t, :])

        ub_bf = sb.tile([P, PACK * L], BF16, name="ub_bf", align_bytes=64)
        ub_v = ub_bf[:].rearrange("p (c t) -> p c t", t=PACK)
        for t, win in enumerate((xb_lo[:, 0, :], xb_lo[:, 1, :], xb_2[:], xb_3[:])):
            nc.vector.tensor_copy(ub_v[:, :, t], win.indirect(l2[:]))
        ub_q = sb.tile([P, L], I32, name="ub_q", align_bytes=64)
        ub_s = sb.tile([P, L], U8, name="ub_s", align_bytes=64)
        nc.vector.quantize_mx(out=ub_q[:].bitcast(E5M2), scales=ub_s[:], in_=ub_bf[:])
        pb = [ps.tile([P, L], F32, name=f"pb{t}") for t in range(PACK)]
        for t in range(PACK):
            cols = slice(t * P, (t + 1) * P)
            nc.tensor.matmul_mx(
                out=pb[t][:], lhsT=w_q[:, cols].bitcast(E5M2), lhsT_scale=ws_q[:, cols],
                rhs=ub_q[:].bitcast(E5M2), rhs_scale=ub_s[:], start=True, stop=True,
            )
        deal(wb_q[:].bitcast(U16), wb_raw[:].bitcast(U16), 8)
        deal(wbs_q[:], wbs_raw[:], 16)
        for t in range(PACK):
            if t % 2 == 0:
                nc.scalar.copy(a[t][:, L:J], pb[t][:])
            else:
                nc.vector.tensor_copy(a[t][:, L:J], pb[t][:])

        g3 = sb.tile([P, PACK, O], F32, name="g3")
        g4 = sb.tile([P, PACK, O], F32, name="g4")
        for t in range(PACK):
            for g, lst in ((g3, l3), (g4, l4)):
                if t % 2 == 0:
                    nc.scalar.activation(g[:, t, :], a[t][:].indirect(lst[:]), COPY)
                else:
                    nc.vector.tensor_copy(g[:, t, :], a[t][:].indirect(lst[:]))
        h_bf = sb.tile([P, PACK * O], BF16, name="h_bf", align_bytes=64)
        nc.vector.tensor_tensor(woven(h_bf), planar(g3), planar(g4), ALU.max)
        h_q = sb.tile([P, O], I32, name="h_q", align_bytes=64)
        h_s = sb.tile([P, O], U8, name="h_s", align_bytes=64)
        nc.vector.quantize_mx(out=h_q[:].bitcast(E5M2), scales=h_s[:], in_=h_bf[:])

        pp = [ps.tile([P, 2, O], F32, name=f"pp{u}") for u in range(2)]
        for t in range(PACK):
            nc.tensor.matmul_mx(
                out=pp[t // 2][:, t % 2, :], lhsT=wb_q[:, 2 * t * P : 2 * (t + 1) * P].bitcast(E2M1),
                lhsT_scale=wbs_q[:, t * P : (t + 1) * P],
                rhs=h_q[:].bitcast(E5M2), rhs_scale=h_s[:], start=True, stop=True,
            )
        y = sb.tile([P, PACK, O], F32, name="y")
        for u in range(2):
            nc.vector.scalar_tensor_tensor(
                y[:, 2 * u : 2 * u + 2, :], rs_sb[:, 2 * u : 2 * u + 2, :], 0.5, pp[u][:], ALU.mult, ALU.add
            )
        for u in range(2):
            nc.vector.scalar_tensor_tensor(
                y[:, 2 * u : 2 * u + 2, 1:O], pp[u][:, :, 0 : O - 1], -0.7, y[:, 2 * u : 2 * u + 2, 1:O], ALU.mult, ALU.add
            )
        nc.sync.dma_start(out_0.rearrange("(p t) o -> p t o", t=PACK), y[:])

        y_bf = sb.tile([P, PACK * O], BF16, name="y_bf", align_bytes=64)
        nc.vector.tensor_copy(woven(y_bf), planar(y))
        y_q = sb.tile([P, O], I32, name="y_q", align_bytes=64)
        y_s = sb.tile([P, O], U8, name="y_s", align_bytes=64)
        nc.vector.quantize_mx(out=y_q[:].bitcast(E4M3), scales=y_s[:], in_=y_bf[:])
        nc.sync.dma_start(out_1[0].rearrange("p c r -> p (c r)").bitcast(I32), y_q[:])
        for q in range(4):
            eng = nc.scalar if q % 2 == 0 else nc.sync
            eng.dma_start(out_2[0, 4 * q : 4 * q + 4, :].bitcast(I32), y_s[32 * q : 32 * q + 4, :].bitcast(I32))
